import numpy as np
import ml_dtypes

BF16 = ml_dtypes.bfloat16


def bf(x):
    return np.asarray(x, np.float32).astype(BF16)


def f32(x):
    return np.asarray(x, np.float32)


def f64(x):
    return np.asarray(x).astype(np.float64)


def striped(idx):
    return np.tile(idx.reshape(-1, 16).T, (8, 1))


S, K, M, N, V = 2048, 128, 256, 256, 128


def setup_inputs():
    return {"table": bf(np.random.standard_normal((K, S))), "w": bf(np.random.standard_normal((K, M)) / np.sqrt(K)), "s": f32(0.5 + np.random.random_sample((M, 1))), "offs": striped(np.random.permutation(S)[:N])}


def reference(table, w, s, offs):
    idx = offs[:16].T.reshape(-1)
    x = f64(table)[:, idx]
    p = f64(w).T @ x[:, :V]
    q = f64(w).T @ x[:, V:]
    return np.abs(p - q) * f64(s)

@@ -1,0 +1,43 @@
+import concourse.mybir as mybir
+
+P = 128
+BF16, F32, U16 = mybir.dt.bfloat16, mybir.dt.float32, mybir.dt.uint16
+ALU = mybir.AluOpType
+
+FLOPS = 2 * 128 * 256 * 256 + 3 * 256 * 128
+
+
+def tile_rows_pair_absd_sub_kernel(tc, table, w, s, offs, out):
+    nc = tc.nc
+    nodes = table.shape[1]
+    features, pairs = out.shape
+    blocks = features // P
+
+    with (
+        tc.tile_pool(name="held", bufs=1) as held,
+        tc.tile_pool(name="work", bufs=blocks) as work,
+        tc.psum_pool(name="psum", bufs=blocks) as psum,
+    ):
+        table_sb = held.tile([P, nodes], BF16)
+        w_sb = held.tile([P, features], BF16)
+        offsets = held.tile([P, offs.shape[1]], U16)
+        s_sb = held.tile([P, blocks], F32)
+
+        nc.sync.dma_start(table_sb[:], table)
+        nc.sync.dma_start(offsets[:], offs)
+        nc.scalar.dma_start(w_sb[:], w)
+        nc.sync.dma_start(s_sb[:], s.rearrange("(b p) o -> p (b o)", p=P))
+
+        for b in range(blocks):
+            pq = psum.tile([P, 2 * pairs], F32)
+            nc.tensor.matmul(pq[:], w_sb[:, b * P:(b + 1) * P], table_sb[:].indirect(offsets[:]),
+                             start=True, stop=True)
+            q_sb = work.tile([P, pairs], F32)
+            nc.vector.tensor_copy(q_sb[:], pq[:, pairs:])
+            diff = work.tile([P, pairs], F32)
+            nc.vector.tensor_tensor(diff[:], pq[:, :pairs], q_sb[:], ALU.subtract)
+            magnitude = work.tile([P, pairs], F32)
+            nc.vector.scalar_tensor_tensor(magnitude[:], diff[:], -1.0, diff[:], ALU.mult, ALU.max)
+            result = work.tile([P, pairs], F32)
+            nc.vector.tensor_scalar(result[:], magnitude[:], s_sb[:, b:b + 1], None, ALU.mult)
+            nc.sync.dma_start(out[b * P:(b + 1) * P, :], result[:])

@@ -1,7 +1,9 @@
 import concourse.mybir as mybir
 
 P = 128
-BF16, F32, U16 = mybir.dt.bfloat16, mybir.dt.float32, mybir.dt.uint16
+BF16, F32, U16, I32 = mybir.dt.bfloat16, mybir.dt.float32, mybir.dt.uint16, mybir.dt.int32
+SIGN_BIT = -0x80000000
+MAGNITUDE_BITS = 0x7FFFFFFF
 ALU = mybir.AluOpType
 
 FLOPS = 2 * 128 * 256 * 256 + 3 * 256 * 128
@@ -28,16 +30,29 @@ def tile_rows_pair_absd_sub_kernel(tc, table, w, s, offs, out):
         nc.scalar.dma_start(w_sb[:], w)
         nc.sync.dma_start(s_sb[:], s.rearrange("(b p) o -> p (b o)", p=P))
 
+        half = offs.shape[1] // 2
+        first_nodes = table_sb[:].indirect(offsets[:, :half])
+        second_nodes = table_sb[:].indirect(offsets[:, half:])
+
+        s_sign = held.tile([P, blocks], I32)
+        nc.vector.tensor_scalar(s_sign[:], s_sb[:].bitcast(I32), SIGN_BIT, None, ALU.bitwise_and)
+
+        scaled_q = []
         for b in range(blocks):
-            pq = psum.tile([P, 2 * pairs], F32)
-            nc.tensor.matmul(pq[:], w_sb[:, b * P:(b + 1) * P], table_sb[:].indirect(offsets[:]),
-                             start=True, stop=True)
-            q_sb = work.tile([P, pairs], F32)
-            nc.vector.tensor_copy(q_sb[:], pq[:, pairs:])
+            q = psum.tile([P, pairs], F32)
+            nc.tensor.matmul(q[:], w_sb[:, b * P:(b + 1) * P], second_nodes, start=True, stop=True)
+            sq = work.tile([P, pairs], F32)
+            nc.vector.tensor_scalar(sq[:], q[:], s_sb[:, b:b + 1], None, ALU.mult)
+            scaled_q.append(sq)
+
+        for b in range(blocks):
+            p = psum.tile([P, pairs], F32)
+            nc.tensor.matmul(p[:], w_sb[:, b * P:(b + 1) * P], first_nodes, start=True, stop=True)
             diff = work.tile([P, pairs], F32)
-            nc.vector.tensor_tensor(diff[:], pq[:, :pairs], q_sb[:], ALU.subtract)
-            magnitude = work.tile([P, pairs], F32)
-            nc.vector.scalar_tensor_tensor(magnitude[:], diff[:], -1.0, diff[:], ALU.mult, ALU.max)
+            nc.vector.scalar_tensor_tensor(diff[:], p[:], s_sb[:, b:b + 1], scaled_q[b][:],
+                                           ALU.mult, ALU.subtract)
             result = work.tile([P, pairs], F32)
-            nc.vector.tensor_scalar(result[:], magnitude[:], s_sb[:, b:b + 1], None, ALU.mult)
+            nc.vector.scalar_tensor_tensor(result[:].bitcast(I32), diff[:].bitcast(I32), MAGNITUDE_BITS,
+                                           s_sign[:, b:b + 1].to_broadcast([P, pairs]),
+                                           ALU.bitwise_and, ALU.bitwise_or)
             nc.sync.dma_start(out[b * P:(b + 1) * P, :], result[:])

import concourse.mybir as mybir

P = 128
BF16, F32, U16, I32 = mybir.dt.bfloat16, mybir.dt.float32, mybir.dt.uint16, mybir.dt.int32
SIGN_BIT = -0x80000000
MAGNITUDE_BITS = 0x7FFFFFFF
ALU = mybir.AluOpType

FLOPS = 2 * 128 * 256 * 256 + 3 * 256 * 128


def tile_rows_pair_absd_sub_kernel(tc, table, w, s, offs, out):
    nc = tc.nc
    nodes = table.shape[1]
    features, pairs = out.shape
    blocks = features // P

    with (
        tc.tile_pool(name="held", bufs=1) as held,
        tc.tile_pool(name="work", bufs=blocks) as work,
        tc.psum_pool(name="psum", bufs=blocks) as psum,
    ):
        table_sb = held.tile([P, nodes], BF16)
        w_sb = held.tile([P, features], BF16)
        offsets = held.tile([P, offs.shape[1]], U16)
        s_sb = held.tile([P, blocks], F32)

        nc.sync.dma_start(table_sb[:], table)
        nc.sync.dma_start(offsets[:], offs)
        nc.scalar.dma_start(w_sb[:], w)
        nc.sync.dma_start(s_sb[:], s.rearrange("(b p) o -> p (b o)", p=P))

        half = offs.shape[1] // 2
        first_nodes = table_sb[:].indirect(offsets[:, :half])
        second_nodes = table_sb[:].indirect(offsets[:, half:])

        s_sign = held.tile([P, blocks], I32)
        nc.vector.tensor_scalar(s_sign[:], s_sb[:].bitcast(I32), SIGN_BIT, None, ALU.bitwise_and)

        scaled_q = []
        for b in range(blocks):
            q = psum.tile([P, pairs], F32)
            nc.tensor.matmul(q[:], w_sb[:, b * P:(b + 1) * P], second_nodes, start=True, stop=True)
            sq = work.tile([P, pairs], F32)
            nc.vector.tensor_scalar(sq[:], q[:], s_sb[:, b:b + 1], None, ALU.mult)
            scaled_q.append(sq)

        for b in range(blocks):
            p = psum.tile([P, pairs], F32)
            nc.tensor.matmul(p[:], w_sb[:, b * P:(b + 1) * P], first_nodes, start=True, stop=True)
            diff = work.tile([P, pairs], F32)
            nc.vector.scalar_tensor_tensor(diff[:], p[:], s_sb[:, b:b + 1], scaled_q[b][:],
                                           ALU.mult, ALU.subtract)
            result = work.tile([P, pairs], F32)
            nc.vector.scalar_tensor_tensor(result[:].bitcast(I32), diff[:].bitcast(I32), MAGNITUDE_BITS,
                                           s_sign[:, b:b + 1].to_broadcast([P, pairs]),
                                           ALU.bitwise_and, ALU.bitwise_or)
            nc.sync.dma_start(out[b * P:(b + 1) * P, :], result[:])
